import numpy as np
import ml_dtypes


def mxq(x, axis, fmt="e4m3"):
    dtype, down = {"e4m3": (ml_dtypes.float8_e4m3fn, 7), "e5m2": (ml_dtypes.float8_e5m2, 14)}[fmt]
    v = np.moveaxis(np.asarray(x, np.float32).astype(ml_dtypes.bfloat16).astype(np.float64), axis, -1)
    blocks = v.reshape(v.shape[:-1] + (-1, 32))
    amax = np.abs(blocks).max(-1, keepdims=True)
    byte = np.maximum(np.where(amax > 0, np.frexp(amax)[1] - 1 + 127, 0) - down, 1)
    scale = np.exp2(byte - 127.0)
    codes = (blocks / scale).astype(np.float32).astype(dtype).astype(np.float64)
    return np.moveaxis((codes * scale).reshape(v.shape), -1, axis)


WIDE = False


def mx_kscale(k):
    if not WIDE:
        return np.ones(k)
    levels = np.array([30, -30])
    if k % 512:
        return np.exp2(np.random.permutation(np.resize(levels, k // 32))).repeat(32)
    a = np.empty((k // 512, 16))
    for p in range(k // 512):
        a[p, :8] = np.random.permutation(np.resize(levels, 8))
        for g in range(8):
            far = levels[np.abs(levels - a[p, g]) >= 10]
            a[p, g + 8] = far[np.random.randint(len(far))]
    return np.exp2(a.ravel()).repeat(32)


def f64(x):
    return np.asarray(x).astype(np.float64)


def striped(idx):
    return np.tile(np.asarray(idx).reshape(-1, 16).T, (8, 1)).astype(np.uint16)


def unstriped(offs):
    return offs[:16].T.reshape(-1).astype(np.int64)


E2M1 = np.array([0.0, 0.5, 1.0, 1.5, 2.0, 3.0, 4.0, 6.0, -0.0, -0.5, -1.0, -1.5, -2.0, -3.0, -4.0, -6.0])


def pack_weight(w, fmt):
    k, n = w.shape
    w = f64(np.asarray(w, np.float32).astype(ml_dtypes.bfloat16)).reshape(k // 32, 32, n)
    amax = np.abs(w).max(1)
    if fmt in ("e4m3", "e5m2"):
        byte = np.frexp(amax)[1] - 1 + 127 - (7 if fmt == "e4m3" else 14)
    else:
        mant, ex = np.frexp(amax / 6.0)
        byte = np.where(mant > 0.5, ex, ex - 1) + 127
    byte = np.clip(np.where(amax > 0, byte, 1), 1, 254)
    scaled = (w * np.exp2(127.0 - byte)[:, None, :]).reshape(k, n).astype(np.float32)
    by_word = np.ascontiguousarray(scaled.reshape(k // 512, 128, 4, n).transpose(0, 1, 3, 2))
    if fmt in ("e4m3", "e5m2"):
        words = by_word.astype(ml_dtypes.float8_e4m3fn if fmt == "e4m3" else ml_dtypes.float8_e5m2).view(np.uint8)
    else:
        c = by_word.astype(ml_dtypes.float4_e2m1fn).view(np.uint8) & 0xF
        words = (c[..., 0::2] | (c[..., 1::2] << 4)).reshape(k // 512, 128, 2 * n)
    return np.ascontiguousarray(words), np.ascontiguousarray(byte.astype(np.uint8).reshape(k // 512, 16, n))


def unpack_weight(words, scales, fmt):
    g, _, n = scales.shape
    words = np.ascontiguousarray(words).reshape(g, 128, n, -1)
    if fmt in ("e4m3", "e5m2"):
        vals = words.view(ml_dtypes.float8_e4m3fn if fmt == "e4m3" else ml_dtypes.float8_e5m2).astype(np.float64)
    else:
        nib = np.empty((g, 128, n, 4), np.uint8)
        nib[..., 0::2] = words & 0xF
        nib[..., 1::2] = words >> 4
        vals = E2M1[nib]
    vals = vals * np.repeat(np.exp2(scales.astype(np.float64) - 127.0), 8, axis=1)[..., None]
    return vals.transpose(0, 1, 3, 2).reshape(g * 512, n)


K, T, I, J, N, Z, S, V, E = 512, 1024, 512, 256, 256, 1024, 1024, 1024, 128


def setup_inputs():
    n = np.random.standard_normal
    idx = np.random.permutation(T)[:I]
    idx2 = np.random.permutation(Z)[:J]
    idx3 = np.random.permutation(V)[:J]
    idx4 = np.random.permutation(S)[:N]
    idx5 = np.random.permutation(J)[:E]
    idx6 = np.random.permutation(J)[:E]
    fk = mx_kscale(K)
    fi = mx_kscale(I)
    ti = np.ones(T)
    ti[idx] = fi
    xkp = pack_weight(n((K, T)) * 0.3 * fk[:, None] * ti, "e2m1")
    xqp = pack_weight(n((K, Z)) * 0.3 / fk[:, None], "e5m2")
    xrp = pack_weight(n((K, V)) * 0.3 / fk[:, None], "e4m3")
    vsp = pack_weight(n((I, S)) / fi[:, None], "e2m1")
    return {
        "xk_words": xkp[0],
        "xk_scales": xkp[1],
        "xq_words": xqp[0],
        "xq_scales": xqp[1],
        "xr_words": xrp[0],
        "xr_scales": xrp[1],
        "vs_words": vsp[0],
        "vs_scales": vsp[1],
        "offs": striped(idx),
        "offs2": striped(idx2),
        "offs3": striped(idx3),
        "offs4": striped(idx4),
        "offs5": striped(idx5),
        "offs6": striped(idx6),
    }


def reference(xk_words, xk_scales, xq_words, xq_scales, xr_words, xr_scales, vs_words, vs_scales, offs, offs2, offs3, offs4, offs5, offs6):
    idx = unstriped(offs)
    idx2 = unstriped(offs2)
    idx3 = unstriped(offs3)
    idx4 = unstriped(offs4)
    idx5 = unstriped(offs5)
    idx6 = unstriped(offs6)
    xku = unpack_weight(xk_words, xk_scales, "e2m1")
    xqu = unpack_weight(xq_words, xq_scales, "e5m2")
    xru = unpack_weight(xr_words, xr_scales, "e4m3")
    vsu = unpack_weight(vs_words, vs_scales, "e2m1")
    xkidxg = xku[:, idx]
    xqidx2g = xqu[:, idx2]
    s1 = xkidxg.T @ xqidx2g
    xridx3g = xru[:, idx3]
    s2 = xkidxg.T @ xridx3g
    hid = np.abs(s1 - s2)
    vsidx4g = vsu[:, idx4]
    hidq = mxq(hid, 0, "e5m2")
    p = vsidx4g.T @ hidq
    y = np.maximum(p[:, idx5], p[:, idx6])
    return y

@@ -1,0 +1,179 @@
+from contextlib import ExitStack
+
+import concourse.mybir as mybir
+
+K, T, I, J, N, E = 512, 1024, 512, 256, 256, 128
+FLOPS = 2 * K * I * J * 2 + 2 * I * N * J
+
+F32 = mybir.dt.float32
+BF16 = mybir.dt.bfloat16
+I32 = mybir.dt.int32
+U32 = mybir.dt.uint32
+U16 = mybir.dt.uint16
+U8 = mybir.dt.uint8
+E4M3 = mybir.dt.float8_e4m3fn_x4
+E5M2 = mybir.dt.float8_e5m2_x4
+E2M1 = mybir.dt.float4_e2m1fn_x4
+ACT = mybir.ActivationFunctionType
+ALU = mybir.AluOpType
+
+P = 128
+PACK = 4
+CHUNK = 128
+LANES = 16
+
+
+def tile_list_contest_rivals_direct_bestoftwo_kernel(
+    tc, xk_words, xk_scales, xq_words, xq_scales, xr_words, xr_scales, vs_words, vs_scales,
+    offs, offs2, offs3, offs4, offs5, offs6, out,
+):
+    nc = tc.nc
+    chunks = J // CHUNK
+    halves = N // P
+
+    with ExitStack() as ctx:
+        lists = ctx.enter_context(tc.tile_pool(name="lists", bufs=1))
+        sb = ctx.enter_context(tc.tile_pool(name="sb", bufs=1))
+        ps = ctx.enter_context(tc.psum_pool(name="ps", bufs=1))
+
+        def tile(shape, dtype, name):
+            return sb.tile(shape, dtype, name=name, align_bytes=64)
+
+        def load_list(src, name):
+            t = lists.tile(list(src.shape), U16, name=name)
+            nc.sync.dma_start(t[:], src)
+            return t
+
+        def load_words(rows, dtype, name):
+            t = tile([P, T], dtype, name)
+            nc.sync.dma_start(t[:].bitcast(I32), rows.bitcast(I32))
+            return t
+
+        def zeroed_plane(name, engine):
+            t = tile([P, T], U8, name)
+            engine.memset(t[:].bitcast(I32), 0)
+            return t
+
+        def load_rows(t, src, a, queue):
+            queue.dma_start(t[32 * a : 32 * a + 4, :].bitcast(I32), src[0, 4 * a : 4 * a + 4, :].bitcast(I32))
+
+        def load_rows_repeated(t, src, a, queue):
+            rows = src[0, 4 * a : 4 * a + 4, :].bitcast(I32).unsqueeze(0).broadcast_to([8, 4, T // 4])
+            queue.dma_start(t[32 * a : 32 * a + 32, :].bitcast(I32), rows)
+
+        def gather(dst, window, offsets):
+            nc.vector.tensor_copy(dst, window[:].indirect(offsets))
+
+        xr_s = zeroed_plane("xr_s", nc.vector)
+        xq_s = zeroed_plane("xq_s", nc.gpsimd)
+        vs_s = zeroed_plane("vs_s", nc.vector)
+
+        xk_s = tile([P, T], U8, "xk_s")
+        for a in range(3):
+            load_rows_repeated(xk_s, xk_scales, a, nc.scalar)
+        load_rows(xr_s, xr_scales, 0, nc.scalar)
+        xk_w = load_words(xk_words[0], U16, "xk_w")
+        load_rows_repeated(xk_s, xk_scales, 3, nc.sync)
+        idx = load_list(offs, "idx")
+        xr_w = load_words(xr_words[0].rearrange("p c r -> p (c r)"), U32, "xr_w")
+        for a in range(1, 4):
+            load_rows(xr_s, xr_scales, a, nc.sync)
+        idx3 = load_list(offs3, "idx3")
+        load_rows(xq_s, xq_scales, 0, nc.sync)
+        xq_w = load_words(xq_words[0].rearrange("p c r -> p (c r)"), U32, "xq_w")
+        for a in range(1, 4):
+            load_rows(xq_s, xq_scales, a, nc.sync)
+        vs_w = load_words(vs_words[0], U16, "vs_w")
+        for a in range(2):
+            load_rows(vs_s, vs_scales, a, nc.sync)
+        idx2 = load_list(offs2, "idx2")
+        idx4 = load_list(offs4, "idx4")
+        for a in range(2, 4):
+            load_rows(vs_s, vs_scales, a, nc.sync)
+        idx5 = load_list(offs5, "idx5")
+        idx6 = load_list(offs6, "idx6")
+
+        key_listed = tile([P, I], U16, "key_listed")
+        key_w = tile([P, I], U16, "key_w")
+        key_s = tile([P, I], U8, "key_s")
+        gather(key_listed[:], xk_w, idx[:])
+        gather(key_s[:].rearrange("p (t q) -> p q t", t=PACK), xk_s, idx[:])
+        nc.vector.tensor_copy(
+            key_w[:].rearrange("p (t q) -> p t q", t=PACK), key_listed[:].rearrange("p (q t) -> p t q", t=PACK)
+        )
+
+        def scores(c, words, scales, offsets, fmt, name):
+            w = tile([P, CHUNK], U32, name + "_w")
+            s = tile([P, CHUNK], U8, name + "_s")
+            cols = offsets[:, c * CHUNK // LANES : (c + 1) * CHUNK // LANES]
+            gather(w[:], words, cols)
+            gather(s[:], scales, cols)
+            bank = ps.tile([P, PACK, CHUNK], F32, name=name + "_bank")
+            for t in range(PACK):
+                nc.tensor.matmul_mx(
+                    out=bank[:, t, :],
+                    lhsT=key_w[:, t * P : (t + 1) * P].bitcast(E2M1),
+                    lhsT_scale=key_s[:, t * P : (t + 1) * P],
+                    rhs=w[:].bitcast(fmt),
+                    rhs_scale=s[:],
+                    start=True,
+                    stop=True,
+                )
+            return bank[:].rearrange("p t j -> p j t")
+
+        s1, s2 = [], []
+        for c in range(chunks):
+            bank = scores(c, xr_w, xr_s, idx3, E4M3, "rival%d" % c)
+            s2_sb = tile([P, CHUNK, PACK], F32, "s2_%d" % c)
+            nc.scalar.activation(out=s2_sb[:], in_=bank, func=ACT.Copy)
+            s2.append(s2_sb)
+        for c in range(chunks):
+            s1.append(scores(c, xq_w, xq_s, idx2, E5M2, "query%d" % c))
+
+        store_w = tile([P, N], U16, "store_w")
+        store_s = tile([P, N], U8, "store_s")
+        hid = []
+        for c in range(chunks):
+            diff = tile([P, CHUNK, PACK], F32, "diff%d" % c)
+            nc.vector.tensor_tensor(diff[:], s1[c], s2[c][:], ALU.subtract)
+            h = tile([P, CHUNK * PACK], BF16, "hid%d" % c)
+            nc.scalar.activation(out=h[:], in_=diff[:].rearrange("p j t -> p (j t)"), func=ACT.Abs)
+            hid.append(h)
+            if c == 0:
+                gather(store_w[:], vs_w, idx4[:])
+            else:
+                gather(store_s[:], vs_s, idx4[:])
+
+        p_sb = [tile([P, J], F32, "p%d" % h) for h in range(halves)]
+        for c in range(chunks):
+            hid_w = tile([P, CHUNK], U32, "hid_w%d" % c)
+            hid_s = tile([P, CHUNK], U8, "hid_s%d" % c)
+            nc.vector.quantize_mx(out=hid_w[:].bitcast(E5M2), scales=hid_s[:], in_=hid[c][:])
+            for h in range(halves):
+                bank = ps.tile([P, CHUNK], F32, name="p_bank%d%d" % (c, h))
+                nc.tensor.matmul_mx(
+                    out=bank[:],
+                    lhsT=store_w[:, h * P : (h + 1) * P].bitcast(E2M1),
+                    lhsT_scale=store_s[:, h * P : (h + 1) * P],
+                    rhs=hid_w[:].bitcast(E5M2),
+                    rhs_scale=hid_s[:],
+                    start=True,
+                    stop=True,
+                )
+                dst = p_sb[h][:, c * CHUNK : (c + 1) * CHUNK]
+                if h == 0:
+                    nc.scalar.copy(dst, bank[:])
+                else:
+                    nc.vector.tensor_copy(dst, bank[:])
+
+        for h in range(halves):
+            first = tile([P, E], F32, "first%d" % h)
+            second = tile([P, E], F32, "second%d" % h)
+            for dst, offsets in ((first, idx5), (second, idx6)):
+                if h == 0:
+                    nc.scalar.activation(out=dst[:], in_=p_sb[h][:].indirect(offsets[:]), func=ACT.Copy)
+                else:
+                    gather(dst[:], p_sb[h], offsets[:])
+            best = tile([P, E], F32, "best%d" % h)
+            nc.vector.tensor_tensor(best[:], first[:], second[:], ALU.max)
+            nc.sync.dma_start(out[h * P : (h + 1) * P, :], best[:])

@@ -57,37 +57,35 @@ def tile_list_contest_rivals_direct_bestoftwo_kernel(
         def load_rows(t, src, a, queue):
             queue.dma_start(t[32 * a : 32 * a + 4, :].bitcast(I32), src[0, 4 * a : 4 * a + 4, :].bitcast(I32))
 
-        def load_rows_repeated(t, src, a, queue):
-            rows = src[0, 4 * a : 4 * a + 4, :].bitcast(I32).unsqueeze(0).broadcast_to([8, 4, T // 4])
-            queue.dma_start(t[32 * a : 32 * a + 32, :].bitcast(I32), rows)
-
         def gather(dst, window, offsets):
             nc.vector.tensor_copy(dst, window[:].indirect(offsets))
 
-        xr_s = zeroed_plane("xr_s", nc.vector)
-        xq_s = zeroed_plane("xq_s", nc.gpsimd)
-        vs_s = zeroed_plane("vs_s", nc.vector)
+        xk_s = zeroed_plane("xk_s", nc.vector)
+        xr_s = zeroed_plane("xr_s", nc.gpsimd)
+        xq_s = zeroed_plane("xq_s", nc.vector)
+        vs_s = zeroed_plane("vs_s", nc.gpsimd)
 
-        xk_s = tile([P, T], U8, "xk_s")
-        for a in range(3):
-            load_rows_repeated(xk_s, xk_scales, a, nc.scalar)
-        load_rows(xr_s, xr_scales, 0, nc.scalar)
-        xk_w = load_words(xk_words[0], U16, "xk_w")
-        load_rows_repeated(xk_s, xk_scales, 3, nc.sync)
         idx = load_list(offs, "idx")
+        xk_w = load_words(xk_words[0], U16, "xk_w")
+        for a in range(2):
+            load_rows(xk_s, xk_scales, a, nc.scalar)
+        load_rows(xr_s, xr_scales, 0, nc.scalar)
+        for a in range(2, 4):
+            load_rows(xk_s, xk_scales, a, nc.sync)
         xr_w = load_words(xr_words[0].rearrange("p c r -> p (c r)"), U32, "xr_w")
         for a in range(1, 4):
             load_rows(xr_s, xr_scales, a, nc.sync)
         idx3 = load_list(offs3, "idx3")
-        load_rows(xq_s, xq_scales, 0, nc.sync)
-        xq_w = load_words(xq_words[0].rearrange("p c r -> p (c r)"), U32, "xq_w")
-        for a in range(1, 4):
+        for a in range(2):
             load_rows(xq_s, xq_scales, a, nc.sync)
-        vs_w = load_words(vs_words[0], U16, "vs_w")
+        xq_w = load_words(xq_words[0].rearrange("p c r -> p (c r)"), U32, "xq_w")
+        for a in range(2, 4):
+            load_rows(xq_s, xq_scales, a, nc.sync)
         for a in range(2):
             load_rows(vs_s, vs_scales, a, nc.sync)
-        idx2 = load_list(offs2, "idx2")
         idx4 = load_list(offs4, "idx4")
+        idx2 = load_list(offs2, "idx2")
+        vs_w = load_words(vs_words[0], U16, "vs_w")
         for a in range(2, 4):
             load_rows(vs_s, vs_scales, a, nc.sync)
         idx5 = load_list(offs5, "idx5")
@@ -96,11 +94,15 @@ def tile_list_contest_rivals_direct_bestoftwo_kernel(
         key_listed = tile([P, I], U16, "key_listed")
         key_w = tile([P, I], U16, "key_w")
         key_s = tile([P, I], U8, "key_s")
-        gather(key_listed[:], xk_w, idx[:])
+        parts = ((0, 384), (384, I))
+        for lo, hi in parts:
+            gather(key_listed[:, lo:hi], xk_w, idx[:, lo // LANES : hi // LANES])
+        for lo, hi in parts:
+            nc.vector.tensor_copy(
+                key_w[:].rearrange("p (t c i) -> p c t i", t=PACK, i=8)[:, lo // 32 : hi // 32],
+                key_listed[:, lo:hi].rearrange("p (c i t) -> p c t i", t=PACK, i=8),
+            )
         gather(key_s[:].rearrange("p (t q) -> p q t", t=PACK), xk_s, idx[:])
-        nc.vector.tensor_copy(
-            key_w[:].rearrange("p (t q) -> p t q", t=PACK), key_listed[:].rearrange("p (q t) -> p t q", t=PACK)
-        )
 
         def scores(c, words, scales, offsets, fmt, name):
             w = tile([P, CHUNK], U32, name + "_w")
@@ -166,14 +168,12 @@ def tile_list_contest_rivals_direct_bestoftwo_kernel(
                 else:
                     nc.vector.tensor_copy(dst, bank[:])
 
+        first = [tile([P, E], F32, "first%d" % h) for h in range(halves)]
+        second = [tile([P, E], F32, "second%d" % h) for h in range(halves)]
         for h in range(halves):
-            first = tile([P, E], F32, "first%d" % h)
-            second = tile([P, E], F32, "second%d" % h)
-            for dst, offsets in ((first, idx5), (second, idx6)):
-                if h == 0:
-                    nc.scalar.activation(out=dst[:], in_=p_sb[h][:].indirect(offsets[:]), func=ACT.Copy)
-                else:
-                    gather(dst[:], p_sb[h], offsets[:])
+            gather(first[h][:], p_sb[h], idx5[:])
+            nc.scalar.activation(out=second[h][:], in_=p_sb[h][:].indirect(idx6[:]), func=ACT.Copy)
+        for h in range(halves):
             best = tile([P, E], F32, "best%d" % h)
-            nc.vector.tensor_tensor(best[:], first[:], second[:], ALU.max)
+            nc.vector.tensor_tensor(best[:], first[h][:], second[h][:], ALU.max)
             nc.sync.dma_start(out[h * P : (h + 1) * P, :], best[:])

@@ -36,8 +36,8 @@ def tile_list_contest_rivals_direct_bestoftwo_kernel(
         sb = ctx.enter_context(tc.tile_pool(name="sb", bufs=1))
         ps = ctx.enter_context(tc.psum_pool(name="ps", bufs=1))
 
-        def tile(shape, dtype, name):
-            return sb.tile(shape, dtype, name=name, align_bytes=64)
+        def tile(shape, dtype, name, tag=""):
+            return sb.tile(shape, dtype, name=name, tag=tag or name, align_bytes=64)
 
         def load_list(src, name):
             t = lists.tile(list(src.shape), U16, name=name)
@@ -81,12 +81,10 @@ def tile_list_contest_rivals_direct_bestoftwo_kernel(
         xq_w = load_words(xq_words[0].rearrange("p c r -> p (c r)"), U32, "xq_w")
         for a in range(2, 4):
             load_rows(xq_s, xq_scales, a, nc.sync)
-        for a in range(2):
-            load_rows(vs_s, vs_scales, a, nc.sync)
         idx4 = load_list(offs4, "idx4")
         idx2 = load_list(offs2, "idx2")
         vs_w = load_words(vs_words[0], U16, "vs_w")
-        for a in range(2, 4):
+        for a in range(4):
             load_rows(vs_s, vs_scales, a, nc.sync)
         idx5 = load_list(offs5, "idx5")
         idx6 = load_list(offs6, "idx6")
@@ -146,27 +144,34 @@ def tile_list_contest_rivals_direct_bestoftwo_kernel(
             else:
                 gather(store_s[:], vs_s, idx4[:])
 
+        hid_plane = tile([P, J], U8, "hid_plane", "vs_s")
         p_sb = [tile([P, J], F32, "p%d" % h) for h in range(halves)]
         for c in range(chunks):
             hid_w = tile([P, CHUNK], U32, "hid_w%d" % c)
-            hid_s = tile([P, CHUNK], U8, "hid_s%d" % c)
-            nc.vector.quantize_mx(out=hid_w[:].bitcast(E5M2), scales=hid_s[:], in_=hid[c][:])
+            hid_s = hid_plane[:, c * CHUNK : (c + 1) * CHUNK]
+            nc.vector.quantize_mx(out=hid_w[:].bitcast(E5M2), scales=hid_s, in_=hid[c][:])
+            last = c == chunks - 1
+            if last:
+                banks = [ps.tile([P, CHUNK], F32, name="p_bank%d%d" % (c, h))[:] for h in range(halves)]
+            else:
+                shared = ps.tile([P, halves, CHUNK], F32, name="p_bank%d" % c)
+                banks = [shared[:, h, :] for h in range(halves)]
             for h in range(halves):
-                bank = ps.tile([P, CHUNK], F32, name="p_bank%d%d" % (c, h))
                 nc.tensor.matmul_mx(
-                    out=bank[:],
+                    out=banks[h],
                     lhsT=store_w[:, h * P : (h + 1) * P].bitcast(E2M1),
                     lhsT_scale=store_s[:, h * P : (h + 1) * P],
                     rhs=hid_w[:].bitcast(E5M2),
-                    rhs_scale=hid_s[:],
+                    rhs_scale=hid_s,
                     start=True,
                     stop=True,
                 )
+            for h in range(halves):
                 dst = p_sb[h][:, c * CHUNK : (c + 1) * CHUNK]
-                if h == 0:
-                    nc.scalar.copy(dst, bank[:])
+                if last:
+                    nc.scalar.copy(dst, banks[h])
                 else:
-                    nc.vector.tensor_copy(dst, bank[:])
+                    nc.vector.tensor_copy(dst, banks[h])
 
         first = [tile([P, E], F32, "first%d" % h) for h in range(halves)]
         second = [tile([P, E], F32, "second%d" % h) for h in range(halves)]

from contextlib import ExitStack

import concourse.mybir as mybir

K, T, I, J, N, E = 512, 1024, 512, 256, 256, 128
FLOPS = 2 * K * I * J * 2 + 2 * I * N * J

F32 = mybir.dt.float32
BF16 = mybir.dt.bfloat16
I32 = mybir.dt.int32
U32 = mybir.dt.uint32
U16 = mybir.dt.uint16
U8 = mybir.dt.uint8
E4M3 = mybir.dt.float8_e4m3fn_x4
E5M2 = mybir.dt.float8_e5m2_x4
E2M1 = mybir.dt.float4_e2m1fn_x4
ACT = mybir.ActivationFunctionType
ALU = mybir.AluOpType

P = 128
PACK = 4
CHUNK = 128
LANES = 16


def tile_list_contest_rivals_direct_bestoftwo_kernel(
    tc, xk_words, xk_scales, xq_words, xq_scales, xr_words, xr_scales, vs_words, vs_scales,
    offs, offs2, offs3, offs4, offs5, offs6, out,
):
    nc = tc.nc
    chunks = J // CHUNK
    halves = N // P

    with ExitStack() as ctx:
        lists = ctx.enter_context(tc.tile_pool(name="lists", bufs=1))
        sb = ctx.enter_context(tc.tile_pool(name="sb", bufs=1))
        ps = ctx.enter_context(tc.psum_pool(name="ps", bufs=1))

        def tile(shape, dtype, name, tag=""):
            return sb.tile(shape, dtype, name=name, tag=tag or name, align_bytes=64)

        def load_list(src, name):
            t = lists.tile(list(src.shape), U16, name=name)
            nc.sync.dma_start(t[:], src)
            return t

        def load_words(rows, dtype, name):
            t = tile([P, T], dtype, name)
            nc.sync.dma_start(t[:].bitcast(I32), rows.bitcast(I32))
            return t

        def zeroed_plane(name, engine):
            t = tile([P, T], U8, name)
            engine.memset(t[:].bitcast(I32), 0)
            return t

        def load_rows(t, src, a, queue):
            queue.dma_start(t[32 * a : 32 * a + 4, :].bitcast(I32), src[0, 4 * a : 4 * a + 4, :].bitcast(I32))

        def gather(dst, window, offsets):
            nc.vector.tensor_copy(dst, window[:].indirect(offsets))

        xk_s = zeroed_plane("xk_s", nc.vector)
        xr_s = zeroed_plane("xr_s", nc.gpsimd)
        xq_s = zeroed_plane("xq_s", nc.vector)
        vs_s = zeroed_plane("vs_s", nc.gpsimd)

        idx = load_list(offs, "idx")
        xk_w = load_words(xk_words[0], U16, "xk_w")
        for a in range(2):
            load_rows(xk_s, xk_scales, a, nc.scalar)
        load_rows(xr_s, xr_scales, 0, nc.scalar)
        for a in range(2, 4):
            load_rows(xk_s, xk_scales, a, nc.sync)
        xr_w = load_words(xr_words[0].rearrange("p c r -> p (c r)"), U32, "xr_w")
        for a in range(1, 4):
            load_rows(xr_s, xr_scales, a, nc.sync)
        idx3 = load_list(offs3, "idx3")
        for a in range(2):
            load_rows(xq_s, xq_scales, a, nc.sync)
        xq_w = load_words(xq_words[0].rearrange("p c r -> p (c r)"), U32, "xq_w")
        for a in range(2, 4):
            load_rows(xq_s, xq_scales, a, nc.sync)
        idx4 = load_list(offs4, "idx4")
        idx2 = load_list(offs2, "idx2")
        vs_w = load_words(vs_words[0], U16, "vs_w")
        for a in range(4):
            load_rows(vs_s, vs_scales, a, nc.sync)
        idx5 = load_list(offs5, "idx5")
        idx6 = load_list(offs6, "idx6")

        key_listed = tile([P, I], U16, "key_listed")
        key_w = tile([P, I], U16, "key_w")
        key_s = tile([P, I], U8, "key_s")
        parts = ((0, 384), (384, I))
        for lo, hi in parts:
            gather(key_listed[:, lo:hi], xk_w, idx[:, lo // LANES : hi // LANES])
        for lo, hi in parts:
            nc.vector.tensor_copy(
                key_w[:].rearrange("p (t c i) -> p c t i", t=PACK, i=8)[:, lo // 32 : hi // 32],
                key_listed[:, lo:hi].rearrange("p (c i t) -> p c t i", t=PACK, i=8),
            )
        gather(key_s[:].rearrange("p (t q) -> p q t", t=PACK), xk_s, idx[:])

        def scores(c, words, scales, offsets, fmt, name):
            w = tile([P, CHUNK], U32, name + "_w")
            s = tile([P, CHUNK], U8, name + "_s")
            cols = offsets[:, c * CHUNK // LANES : (c + 1) * CHUNK // LANES]
            gather(w[:], words, cols)
            gather(s[:], scales, cols)
            bank = ps.tile([P, PACK, CHUNK], F32, name=name + "_bank")
            for t in range(PACK):
                nc.tensor.matmul_mx(
                    out=bank[:, t, :],
                    lhsT=key_w[:, t * P : (t + 1) * P].bitcast(E2M1),
                    lhsT_scale=key_s[:, t * P : (t + 1) * P],
                    rhs=w[:].bitcast(fmt),
                    rhs_scale=s[:],
                    start=True,
                    stop=True,
                )
            return bank[:].rearrange("p t j -> p j t")

        s1, s2 = [], []
        for c in range(chunks):
            bank = scores(c, xr_w, xr_s, idx3, E4M3, "rival%d" % c)
            s2_sb = tile([P, CHUNK, PACK], F32, "s2_%d" % c)
            nc.scalar.activation(out=s2_sb[:], in_=bank, func=ACT.Copy)
            s2.append(s2_sb)
        for c in range(chunks):
            s1.append(scores(c, xq_w, xq_s, idx2, E5M2, "query%d" % c))

        store_w = tile([P, N], U16, "store_w")
        store_s = tile([P, N], U8, "store_s")
        hid = []
        for c in range(chunks):
            diff = tile([P, CHUNK, PACK], F32, "diff%d" % c)
            nc.vector.tensor_tensor(diff[:], s1[c], s2[c][:], ALU.subtract)
            h = tile([P, CHUNK * PACK], BF16, "hid%d" % c)
            nc.scalar.activation(out=h[:], in_=diff[:].rearrange("p j t -> p (j t)"), func=ACT.Abs)
            hid.append(h)
            if c == 0:
                gather(store_w[:], vs_w, idx4[:])
            else:
                gather(store_s[:], vs_s, idx4[:])

        hid_plane = tile([P, J], U8, "hid_plane", "vs_s")
        p_sb = [tile([P, J], F32, "p%d" % h) for h in range(halves)]
        for c in range(chunks):
            hid_w = tile([P, CHUNK], U32, "hid_w%d" % c)
            hid_s = hid_plane[:, c * CHUNK : (c + 1) * CHUNK]
            nc.vector.quantize_mx(out=hid_w[:].bitcast(E5M2), scales=hid_s, in_=hid[c][:])
            last = c == chunks - 1
            if last:
                banks = [ps.tile([P, CHUNK], F32, name="p_bank%d%d" % (c, h))[:] for h in range(halves)]
            else:
                shared = ps.tile([P, halves, CHUNK], F32, name="p_bank%d" % c)
                banks = [shared[:, h, :] for h in range(halves)]
            for h in range(halves):
                nc.tensor.matmul_mx(
                    out=banks[h],
                    lhsT=store_w[:, h * P : (h + 1) * P].bitcast(E2M1),
                    lhsT_scale=store_s[:, h * P : (h + 1) * P],
                    rhs=hid_w[:].bitcast(E5M2),
                    rhs_scale=hid_s,
                    start=True,
                    stop=True,
                )
            for h in range(halves):
                dst = p_sb[h][:, c * CHUNK : (c + 1) * CHUNK]
                if last:
                    nc.scalar.copy(dst, banks[h])
                else:
                    nc.vector.tensor_copy(dst, banks[h])

        first = [tile([P, E], F32, "first%d" % h) for h in range(halves)]
        second = [tile([P, E], F32, "second%d" % h) for h in range(halves)]
        for h in range(halves):
            gather(first[h][:], p_sb[h], idx5[:])
            nc.scalar.activation(out=second[h][:], in_=p_sb[h][:].indirect(idx6[:]), func=ACT.Copy)
        for h in range(halves):
            best = tile([P, E], F32, "best%d" % h)
            nc.vector.tensor_tensor(best[:], first[h][:], second[h][:], ALU.max)
            nc.sync.dma_start(out[h * P : (h + 1) * P, :], best[:])
